import numpy as np
import ml_dtypes


def mxq(x, axis, fmt="e4m3"):
    dtype, down = {"e4m3": (ml_dtypes.float8_e4m3fn, 7), "e5m2": (ml_dtypes.float8_e5m2, 14)}[fmt]
    v = np.moveaxis(np.asarray(x, np.float32).astype(ml_dtypes.bfloat16).astype(np.float64), axis, -1)
    blocks = v.reshape(v.shape[:-1] + (-1, 32))
    amax = np.abs(blocks).max(-1, keepdims=True)
    byte = np.maximum(np.where(amax > 0, np.frexp(amax)[1] - 1 + 127, 0) - down, 1)
    scale = np.exp2(byte - 127.0)
    codes = (blocks / scale).astype(np.float32).astype(dtype).astype(np.float64)
    return np.moveaxis((codes * scale).reshape(v.shape), -1, axis)


WIDE = False


def mx_kscale(k):
    if not WIDE:
        return np.ones(k)
    levels = np.array([10, -10, 5, -5, 0])
    if k % 512:
        return np.exp2(np.random.permutation(np.resize(levels, k // 32))).repeat(32)
    a = np.empty((k // 512, 16))
    for p in range(k // 512):
        a[p, :8] = np.random.permutation(np.resize(levels, 8))
        for g in range(8):
            far = levels[np.abs(levels - a[p, g]) >= 10]
            a[p, g + 8] = far[np.random.randint(len(far))]
    return np.exp2(a.ravel()).repeat(32)


def f64(x):
    return np.asarray(x).astype(np.float64)


def striped(idx):
    return np.tile(idx.reshape(-1, 16).T, (8, 1)).astype(np.uint16)


def unstriped(offs):
    return offs[:16].T.reshape(-1).astype(np.int64)


def striped8(idx):
    return np.concatenate([x.reshape(-1, 16).T for x in idx]).astype(np.uint16)


def runs(offs, k):
    lists = np.stack([offs[16 * r : 16 * r + 16].T.reshape(-1) for r in range(8)]).astype(np.int64)
    return lists[np.arange(k) % 512 // 64]


def pack_weight(w):
    k, n = w.shape
    w = f64(np.asarray(w, np.float32).astype(ml_dtypes.bfloat16)).reshape(k // 32, 32, n)
    amax = np.abs(w).max(1)
    byte = np.clip(np.where(amax > 0, np.frexp(amax)[1] - 1 + 127 - 7, 1), 1, 254)
    scaled = (w * np.exp2(127.0 - byte)[:, None, :]).reshape(k, n).astype(np.float32)
    words = np.ascontiguousarray(scaled.reshape(k // 512, 128, 4, n).transpose(0, 1, 3, 2)).astype(ml_dtypes.float8_e4m3fn).view(np.uint8)
    return words, np.ascontiguousarray(byte.astype(np.uint8).reshape(k // 512, 16, n))


def unpack_weight(words, scales):
    g, p, n, _ = words.shape
    vals = np.ascontiguousarray(words).view(ml_dtypes.float8_e4m3fn).astype(np.float64) * np.repeat(np.exp2(scales.astype(np.float64) - 127.0), 8, axis=1)[..., None]
    return vals.transpose(0, 1, 3, 2).reshape(g * 512, n)

def planes(y):
    n, m = y.shape
    v = y.astype(np.float32).astype(ml_dtypes.bfloat16).astype(np.float64).reshape(n // 32, 32, m)
    top = np.abs(v).max(1)
    byte = np.clip(np.where(top > 0, np.frexp(top)[1] - 1 + 127 - 7, 1), 1, 254)
    codes = (v * np.exp2(127.0 - byte)[:, None, :]).reshape(n, m).astype(np.float32).astype(ml_dtypes.float8_e4m3fn).view(np.uint8)
    words = codes.reshape(n // 512, 128, 4, m).transpose(0, 1, 3, 2)
    return np.ascontiguousarray(words), np.ascontiguousarray(byte.astype(np.uint8).reshape(n // 512, 16, m))


K, T, S, V, H = 512, 2048, 512, 256, 512


def setup_inputs():
    n = np.random.standard_normal
    s = mx_kscale(K)[:, None]
    u = mx_kscale(S)
    packed_xT = pack_weight(n((K, T)) * s)
    return {
        "x_words": packed_xT[0],
        "x_scales": packed_xT[1],
        "wa": (n((K, H)) / np.sqrt(K) / s).astype(np.float32),
        "wb": (n((K, H)) / np.sqrt(K) / s).astype(np.float32),
        "gt": (np.random.uniform(0.5, 1.5, (S, 1)) * u[:, None]).astype(np.float32),
        "gi": (np.random.uniform(0.5, 1.5, (S, 1)) / u[:, None]).astype(np.float32),
        "offs": striped(np.random.permutation(T)[:S]),
        "fa": striped8(np.stack([np.random.permutation(H)[:V] for _ in range(8)])),
    }


def reference(x_words, x_scales, wa, wb, gt, gi, offs, fa):
    xq = unpack_weight(x_words, x_scales)[:, unstriped(offs)]
    b = xq.T @ mxq(f64(wb), 0, "e4m3")
    z = f64(gt) * b
    a = xq.T @ mxq(f64(wa), 0, "e4m3")
    z2 = f64(gi) * (a[np.arange(S)[:, None], runs(fa, S)])
    out_0 = 0.0625 * ((mxq(z, 0, "e4m3").T @ mxq(z2, 0, "e4m3")))
    return (out_0,) + planes(out_0)

@@ -1,0 +1,209 @@
+from contextlib import ExitStack
+
+import concourse.mybir as mybir
+from concourse.masks import make_identity
+
+K, T, S, V, H = 512, 2048, 512, 256, 512
+FLOPS = 2 * (2 * S * K * H + S * H * V)
+
+F32 = mybir.dt.float32
+BF16 = mybir.dt.bfloat16
+I32 = mybir.dt.int32
+U32 = mybir.dt.uint32
+U16 = mybir.dt.uint16
+U8 = mybir.dt.uint8
+FP8X4 = mybir.dt.float8_e4m3fn_x4
+COPY = mybir.ActivationFunctionType.Copy
+MULT = mybir.AluOpType.mult
+
+P = 128
+PACK = 4
+RUN = 8
+HALF = H // 2
+QUARTER = H // 4
+
+
+def tile_picked_gramsel_none_po_kernel(tc, x_words, x_scales, wa, wb, gt, gi, offs, fa, out_0, out_1, out_2):
+    nc = tc.nc
+    with ExitStack() as ctx:
+        sb = ctx.enter_context(tc.tile_pool(name="sb", bufs=1))
+        psum = ctx.enter_context(tc.psum_pool(name="psum", bufs=1))
+
+        def sbuf(name, shape, dtype, tag=None):
+            return sb.tile(shape, dtype, name=name, tag=tag or name, align_bytes=64)
+
+        def bank(number, name, shape):
+            return psum.tile(shape, F32, name=name, tag="bank%d" % number)
+
+        def quantize(codes, scales, cols, values):
+            nc.vector.quantize_mx(out=codes[:, cols].bitcast(FP8X4), scales=scales[:, cols], in_=values)
+
+        def product(out, lhs, lhs_cols, rhs, rhs_cols):
+            nc.tensor.matmul_mx(
+                out=out,
+                lhsT=lhs[0][:, lhs_cols].bitcast(FP8X4),
+                lhsT_scale=lhs[1][:, lhs_cols],
+                rhs=rhs[0][:, rhs_cols].bitcast(FP8X4),
+                rhs_scale=rhs[1][:, rhs_cols],
+                start=True,
+                stop=True,
+            )
+
+        def weave(copy, dst, src):
+            copy(
+                out=dst.rearrange("p (c i t) -> p c t i", i=4, t=PACK),
+                in_=src.rearrange("p t (c i) -> p c t i", i=4),
+            )
+
+        def cols(number, width):
+            return slice(number * width, (number + 1) * width)
+
+        token_list = sbuf("token_list", [P, S // 16], U16)
+        feature_lists = sbuf("feature_lists", [P, V // 16], U16)
+        all_words = sbuf("all_words", [P, T], I32)
+        all_scales = sbuf("all_scales", [P, T], U8)
+        gate_rows = sbuf("gate_rows", [P, P], F32)
+        identity = sbuf("identity", [P, P], F32)
+
+        nc.vector.memset(all_scales[:].bitcast(I32), 0)
+        nc.gpsimd.memset(gate_rows[:], 0.0)
+        for first_row, gate in ((0, gt), (PACK, gi)):
+            nc.gpsimd.dma_start(
+                out=gate_rows[first_row : first_row + PACK, :].rearrange("t (b r) -> t b r", r=RUN),
+                in_=gate.rearrange("(b t r) o -> t b (r o)", t=PACK, r=RUN),
+            )
+        make_identity(nc, identity[:])
+
+        wa_raw = [sbuf("wa_raw%d" % h, [P, PACK, HALF], F32) for h in range(2)]
+        wb_raw = [sbuf("wb_raw%d" % h, [P, PACK, HALF], F32) for h in range(2)]
+
+        def load_half(tile, w, h):
+            nc.sync.dma_start(out=tile[:], in_=w.rearrange("(p t) n -> p t n", t=PACK)[:, :, cols(h, HALF)])
+
+        load_half(wa_raw[0], wa, 0)
+        nc.sync.dma_start(token_list[:], offs)
+        for q in range(4):
+            nc.sync.dma_start(
+                out=all_scales[32 * q : 32 * q + 4, :].bitcast(I32),
+                in_=x_scales[0, 4 * q : 4 * q + 4, :].bitcast(I32),
+            )
+        load_half(wa_raw[1], wa, 1)
+        nc.sync.dma_start(out=all_words[:], in_=x_words[0].rearrange("p c r -> p (c r)").bitcast(I32))
+        for h in range(2):
+            load_half(wb_raw[h], wb, h)
+        nc.sync.dma_start(feature_lists[:], fa)
+
+        gate_bank = bank(7, "gate_bank", [P, P])
+        nc.tensor.transpose(gate_bank[:], gate_rows[:], identity[:])
+        gates = sbuf("gates", [P, 2 * PACK], F32)
+        nc.scalar.copy(out=gates[:], in_=gate_bank[:, 0 : 2 * PACK])
+
+        wa_mx = (sbuf("wa_codes", [P, H], U32), sbuf("wa_scale", [P, H], U8))
+        wb_mx = (sbuf("wb_codes", [P, H], U32), sbuf("wb_scale", [P, H], U8))
+        wa_bf = [sbuf("wa_bf%d" % h, [P, HALF * PACK], BF16) for h in range(2)]
+        weave(nc.vector.tensor_copy, wa_bf[0][:], wa_raw[0][:])
+        weave(nc.scalar.copy, wa_bf[1][:], wa_raw[1][:])
+
+        x_codes = sbuf("x_codes", [P, S], U32)
+        picked_scales = sbuf("picked_scales", [P, S], U8)
+        x_scale = sbuf("x_scale", [P, S], U8)
+        nc.vector.tensor_copy(out=picked_scales[:], in_=all_scales[:].indirect(token_list[:]))
+        nc.vector.tensor_copy(
+            out=x_scale[:].bitcast(I32).rearrange("p (t b r) -> p t b r", t=PACK, r=RUN // 4),
+            in_=picked_scales[:].bitcast(I32).rearrange("p (b t r) -> p t b r", t=PACK, r=RUN // 4),
+        )
+        for h in range(2):
+            quantize(*wa_mx, cols(h, HALF), wa_bf[h][:])
+        nc.vector.tensor_copy(
+            out=x_codes[:].rearrange("p (t b r) -> p b t r", t=PACK, r=RUN),
+            in_=all_words[:].bitcast(U32).indirect(token_list[:]),
+        )
+        x_mx = (x_codes, x_scale)
+
+        a_rows = []
+        for t in range(PACK):
+            a_bank = bank(t, "a_bank%d" % t, [P, H])
+            product(a_bank[:], x_mx, cols(t, P), wa_mx, slice(0, H))
+            a_row = sbuf("a_row%d" % t, [P, H], F32)
+            nc.scalar.activation(out=a_row[:], in_=a_bank[:], func=COPY, scale=gates[:, PACK + t : PACK + t + 1])
+            a_rows.append(a_row)
+
+        for h in range(2):
+            wb_bf = sbuf("wb_bf%d" % h, [P, HALF * PACK], BF16)
+            weave(nc.vector.tensor_copy, wb_bf[:], wb_raw[h][:])
+            quantize(*wb_mx, cols(h, HALF), wb_bf[:])
+
+        b_banks = []
+        for c in range(4):
+            b_bank = bank(PACK + c, "b_bank%d" % c, [P, PACK, QUARTER])
+            for t in range(PACK):
+                product(b_bank[:, t, :], x_mx, cols(t, P), wb_mx, cols(c, QUARTER))
+            b_banks.append(b_bank)
+
+        z_bf = sbuf("z_bf", [P, H * PACK], BF16)
+        z_view = z_bf[:].rearrange("p (u m t) -> p u m t", u=PACK, t=PACK)
+        z_planes = sbuf("z_planes", [P, PACK, QUARTER], BF16)
+        for t in range(PACK):
+            nc.scalar.activation(
+                out=z_planes[:, t, :].rearrange("p (u m) -> p u m", u=PACK),
+                in_=b_banks[0][:, t, :].rearrange("p (m u) -> p u m", u=PACK),
+                func=COPY,
+                scale=gates[:, t : t + 1],
+            )
+        nc.scalar.copy(
+            out=z_view[:, :, cols(0, QUARTER // PACK), :].rearrange("p u (c i) t -> p u c t i", i=4),
+            in_=z_planes[:].rearrange("p t (u c i) -> p u c t i", u=PACK, i=4),
+        )
+
+        z2_planes = sbuf("z2_planes", [P, PACK, V], BF16)
+        for t in range(PACK):
+            nc.vector.tensor_copy(out=z2_planes[:, t, :], in_=a_rows[t][:].indirect(feature_lists[:]))
+        z2_bf = sbuf("z2_bf", [P, V * PACK], BF16)
+        weave(nc.scalar.copy, z2_bf[:], z2_planes[:])
+
+        gt_spread = gates[:, 0:PACK].unsqueeze(1).unsqueeze(1).to_broadcast([P, PACK, QUARTER // PACK, PACK])
+        for c in range(1, 4):
+            nc.vector.tensor_tensor(
+                out=z_view[:, :, cols(c, QUARTER // PACK), :],
+                in0=b_banks[c][:].rearrange("p t (m u) -> p u m t", u=PACK),
+                in1=gt_spread,
+                op=MULT,
+            )
+
+        z_mx = (sbuf("z_codes", [P, H], U32), sbuf("z_scale", [P, H], U8))
+        z2_mx = (sbuf("z2_codes", [P, V], U32), sbuf("z2_scale", [P, V], U8))
+        quantize(*z2_mx, slice(0, V), z2_bf[:])
+        for u in range(PACK):
+            quantize(*z_mx, cols(u, P), z_bf[:, cols(u, P * PACK)])
+
+        y_codes = sbuf("y_codes", [P, V], U32)
+        y_scale = sbuf("y_scale", [P, V], U8)
+        out_rows = out_0.rearrange("(p u) v -> p u v", u=PACK)
+        y_banks = [bank(h, "y_bank%d" % h, [P, PACK, P]) for h in range(2)]
+        for u in range(PACK):
+            for h in (1, 0):
+                product(y_banks[h][:, u, :], z_mx, cols(u, P), z2_mx, cols(h, P))
+        y = [sbuf("y%d" % h, [P, PACK, P], F32) for h in range(2)]
+        y_bf = [sbuf("y_bf%d" % h, [P, P * PACK], BF16) for h in range(2)]
+        nc.scalar.activation(out=y[0][:], in_=y_banks[0][:], func=COPY, scale=0.0625)
+        nc.vector.tensor_scalar(
+            out=y_bf[1][:].rearrange("p (v u) -> p v u", u=PACK),
+            in0=y_banks[1][:].rearrange("p u v -> p v u"),
+            scalar1=0.0625,
+            scalar2=None,
+            op0=MULT,
+        )
+        nc.scalar.activation(out=y[1][:], in_=y_banks[1][:], func=COPY, scale=0.0625)
+        weave(nc.vector.tensor_copy, y_bf[0][:], y[0][:])
+        for h in range(2):
+            nc.sync.dma_start(out=out_rows[:, :, cols(h, P)], in_=y[h][:])
+        for h in (1, 0):
+            quantize(y_codes, y_scale, cols(h, P), y_bf[h][:])
+
+        nc.sync.dma_start(out=out_1[0].rearrange("p c r -> p (c r)").bitcast(I32), in_=y_codes[:].bitcast(I32))
+        for q in range(4):
+            queue = nc.scalar if q % 2 else nc.sync
+            queue.dma_start(
+                out=out_2[0, 4 * q : 4 * q + 4, :].bitcast(I32),
+                in_=y_scale[32 * q : 32 * q + 4, :].bitcast(I32),
+            )

@@ -67,11 +67,6 @@ def tile_picked_gramsel_none_po_kernel(tc, x_words, x_scales, wa, wb, gt, gi, of
 
         nc.vector.memset(all_scales[:].bitcast(I32), 0)
         nc.gpsimd.memset(gate_rows[:], 0.0)
-        for first_row, gate in ((0, gt), (PACK, gi)):
-            nc.gpsimd.dma_start(
-                out=gate_rows[first_row : first_row + PACK, :].rearrange("t (b r) -> t b r", r=RUN),
-                in_=gate.rearrange("(b t r) o -> t b (r o)", t=PACK, r=RUN),
-            )
         make_identity(nc, identity[:])
 
         wa_raw = [sbuf("wa_raw%d" % h, [P, PACK, HALF], F32) for h in range(2)]
@@ -80,15 +75,20 @@ def tile_picked_gramsel_none_po_kernel(tc, x_words, x_scales, wa, wb, gt, gi, of
         def load_half(tile, w, h):
             nc.sync.dma_start(out=tile[:], in_=w.rearrange("(p t) n -> p t n", t=PACK)[:, :, cols(h, HALF)])
 
-        load_half(wa_raw[0], wa, 0)
         nc.sync.dma_start(token_list[:], offs)
+        nc.sync.dma_start(out=all_words[:], in_=x_words[0].rearrange("p c r -> p (c r)").bitcast(I32))
         for q in range(4):
             nc.sync.dma_start(
                 out=all_scales[32 * q : 32 * q + 4, :].bitcast(I32),
                 in_=x_scales[0, 4 * q : 4 * q + 4, :].bitcast(I32),
             )
-        load_half(wa_raw[1], wa, 1)
-        nc.sync.dma_start(out=all_words[:], in_=x_words[0].rearrange("p c r -> p (c r)").bitcast(I32))
+        for first_row, gate in ((0, gt), (PACK, gi)):
+            nc.sync.dma_start(
+                out=gate_rows[first_row : first_row + PACK, :].rearrange("t (b r) -> t b r", r=RUN),
+                in_=gate.rearrange("(b t r) o -> t b (r o)", t=PACK, r=RUN),
+            )
+        for h in range(2):
+            load_half(wa_raw[h], wa, h)
         for h in range(2):
             load_half(wb_raw[h], wb, h)
         nc.sync.dma_start(feature_lists[:], fa)
@@ -98,27 +98,31 @@ def tile_picked_gramsel_none_po_kernel(tc, x_words, x_scales, wa, wb, gt, gi, of
         gates = sbuf("gates", [P, 2 * PACK], F32)
         nc.scalar.copy(out=gates[:], in_=gate_bank[:, 0 : 2 * PACK])
 
-        wa_mx = (sbuf("wa_codes", [P, H], U32), sbuf("wa_scale", [P, H], U8))
-        wb_mx = (sbuf("wb_codes", [P, H], U32), sbuf("wb_scale", [P, H], U8))
-        wa_bf = [sbuf("wa_bf%d" % h, [P, HALF * PACK], BF16) for h in range(2)]
-        weave(nc.vector.tensor_copy, wa_bf[0][:], wa_raw[0][:])
-        weave(nc.scalar.copy, wa_bf[1][:], wa_raw[1][:])
-
         x_codes = sbuf("x_codes", [P, S], U32)
         picked_scales = sbuf("picked_scales", [P, S], U8)
         x_scale = sbuf("x_scale", [P, S], U8)
+        nc.vector.tensor_copy(
+            out=x_codes[:].rearrange("p (t b r) -> p b t r", t=PACK, r=RUN),
+            in_=all_words[:].bitcast(U32).indirect(token_list[:]),
+        )
         nc.vector.tensor_copy(out=picked_scales[:], in_=all_scales[:].indirect(token_list[:]))
         nc.vector.tensor_copy(
             out=x_scale[:].bitcast(I32).rearrange("p (t b r) -> p t b r", t=PACK, r=RUN // 4),
             in_=picked_scales[:].bitcast(I32).rearrange("p (b t r) -> p t b r", t=PACK, r=RUN // 4),
         )
-        for h in range(2):
-            quantize(*wa_mx, cols(h, HALF), wa_bf[h][:])
-        nc.vector.tensor_copy(
-            out=x_codes[:].rearrange("p (t b r) -> p b t r", t=PACK, r=RUN),
-            in_=all_words[:].bitcast(U32).indirect(token_list[:]),
-        )
         x_mx = (x_codes, x_scale)
+
+        wa_mx = (sbuf("wa_codes", [P, H], U32), sbuf("wa_scale", [P, H], U8))
+        wb_mx = (sbuf("wb_codes", [P, H], U32), sbuf("wb_scale", [P, H], U8))
+        wa_first = sbuf("wa_first", [P, HALF * PACK], BF16)
+        wa_third = sbuf("wa_third", [P, QUARTER * PACK], BF16)
+        wa_fourth = sbuf("wa_fourth", [P, QUARTER * PACK], BF16)
+        weave(nc.scalar.copy, wa_first[:], wa_raw[0][:])
+        weave(nc.vector.tensor_copy, wa_third[:], wa_raw[1][:, :, cols(0, QUARTER)])
+        weave(nc.scalar.copy, wa_fourth[:], wa_raw[1][:, :, cols(1, QUARTER)])
+        quantize(*wa_mx, cols(0, HALF), wa_first[:])
+        quantize(*wa_mx, cols(2, QUARTER), wa_third[:])
+        quantize(*wa_mx, cols(3, QUARTER), wa_fourth[:])
 
         a_rows = []
         for t in range(PACK):
@@ -128,47 +132,54 @@ def tile_picked_gramsel_none_po_kernel(tc, x_words, x_scales, wa, wb, gt, gi, of
             nc.scalar.activation(out=a_row[:], in_=a_bank[:], func=COPY, scale=gates[:, PACK + t : PACK + t + 1])
             a_rows.append(a_row)
 
-        for h in range(2):
-            wb_bf = sbuf("wb_bf%d" % h, [P, HALF * PACK], BF16)
-            weave(nc.vector.tensor_copy, wb_bf[:], wb_raw[h][:])
-            quantize(*wb_mx, cols(h, HALF), wb_bf[:])
+        wb_first = sbuf("wb_first", [P, QUARTER * PACK], BF16)
+        wb_second = sbuf("wb_second", [P, QUARTER * PACK], BF16, "wa_fourth")
+        wb_last = sbuf("wb_last", [P, HALF * PACK], BF16)
+        weave(nc.scalar.copy, wb_first[:], wb_raw[0][:, :, cols(0, QUARTER)])
+        weave(nc.vector.tensor_copy, wb_second[:], wb_raw[0][:, :, cols(1, QUARTER)])
+        quantize(*wb_mx, cols(0, QUARTER), wb_first[:])
+        quantize(*wb_mx, cols(1, QUARTER), wb_second[:])
+        weave(nc.vector.tensor_copy, wb_last[:], wb_raw[1][:])
+        quantize(*wb_mx, cols(1, HALF), wb_last[:])
 
-        b_banks = []
-        for c in range(4):
-            b_bank = bank(PACK + c, "b_bank%d" % c, [P, PACK, QUARTER])
+        pair_banks = [bank(PACK + pair, "pair_bank%d" % pair, [P, 2, HALF]) for pair in range(2)]
+        for t in range(PACK):
+            product(pair_banks[t // 2][:, t % 2, :], x_mx, cols(t, P), wb_mx, cols(0, HALF))
+        quarter_banks = {}
+        for c in (2, 3):
+            quarter_banks[c] = bank(PACK + c, "quarter_bank%d" % c, [P, PACK, QUARTER])
             for t in range(PACK):
-                product(b_bank[:, t, :], x_mx, cols(t, P), wb_mx, cols(c, QUARTER))
-            b_banks.append(b_bank)
+                product(quarter_banks[c][:, t, :], x_mx, cols(t, P), wb_mx, cols(c, QUARTER))
 
-        z_bf = sbuf("z_bf", [P, H * PACK], BF16)
-        z_view = z_bf[:].rearrange("p (u m t) -> p u m t", u=PACK, t=PACK)
-        z_planes = sbuf("z_planes", [P, PACK, QUARTER], BF16)
+        z2_planes = sbuf("z2_planes", [P, PACK, V], BF16, "wb_raw1")
+        for t in range(PACK):
+            nc.vector.tensor_copy(out=z2_planes[:, t, :], in_=a_rows[t][:].indirect(feature_lists[:]))
+        z_planes = sbuf("z_planes", [P, PACK, HALF], BF16, "a_row0")
         for t in range(PACK):
             nc.scalar.activation(
                 out=z_planes[:, t, :].rearrange("p (u m) -> p u m", u=PACK),
-                in_=b_banks[0][:, t, :].rearrange("p (m u) -> p u m", u=PACK),
+                in_=pair_banks[t // 2][:, t % 2, :].rearrange("p (m u) -> p u m", u=PACK),
                 func=COPY,
                 scale=gates[:, t : t + 1],
             )
-        nc.scalar.copy(
-            out=z_view[:, :, cols(0, QUARTER // PACK), :].rearrange("p u (c i) t -> p u c t i", i=4),
-            in_=z_planes[:].rearrange("p t (u c i) -> p u c t i", u=PACK, i=4),
-        )
 
-        z2_planes = sbuf("z2_planes", [P, PACK, V], BF16)
-        for t in range(PACK):
-            nc.vector.tensor_copy(out=z2_planes[:, t, :], in_=a_rows[t][:].indirect(feature_lists[:]))
         z2_bf = sbuf("z2_bf", [P, V * PACK], BF16)
         weave(nc.scalar.copy, z2_bf[:], z2_planes[:])
 
+        z_bf = sbuf("z_bf", [P, H * PACK], BF16, "a_row3")
+        z_view = z_bf[:].rearrange("p (u m t) -> p u m t", u=PACK, t=PACK)
         gt_spread = gates[:, 0:PACK].unsqueeze(1).unsqueeze(1).to_broadcast([P, PACK, QUARTER // PACK, PACK])
-        for c in range(1, 4):
+        for c in (2, 3):
             nc.vector.tensor_tensor(
                 out=z_view[:, :, cols(c, QUARTER // PACK), :],
-                in0=b_banks[c][:].rearrange("p t (m u) -> p u m t", u=PACK),
+                in0=quarter_banks[c][:].rearrange("p t (m u) -> p u m t", u=PACK),
                 in1=gt_spread,
                 op=MULT,
             )
+        nc.vector.tensor_copy(
+            out=z_view[:, :, cols(0, HALF // PACK), :].rearrange("p u (c i) t -> p u c t i", i=4),
+            in_=z_planes[:].rearrange("p t (u c i) -> p u c t i", u=PACK, i=4),
+        )
 
         z_mx = (sbuf("z_codes", [P, H], U32), sbuf("z_scale", [P, H], U8))
         z2_mx = (sbuf("z2_codes", [P, V], U32), sbuf("z2_scale", [P, V], U8))
@@ -179,25 +190,17 @@ def tile_picked_gramsel_none_po_kernel(tc, x_words, x_scales, wa, wb, gt, gi, of
         y_codes = sbuf("y_codes", [P, V], U32)
         y_scale = sbuf("y_scale", [P, V], U8)
         out_rows = out_0.rearrange("(p u) v -> p u v", u=PACK)
-        y_banks = [bank(h, "y_bank%d" % h, [P, PACK, P]) for h in range(2)]
+        y = sbuf("y", [P, PACK, V], F32)
         for u in range(PACK):
-            for h in (1, 0):
-                product(y_banks[h][:, u, :], z_mx, cols(u, P), z2_mx, cols(h, P))
-        y = [sbuf("y%d" % h, [P, PACK, P], F32) for h in range(2)]
+            y_bank = bank(u, "y_bank%d" % u, [P, V])
+            product(y_bank[:], z_mx, cols(u, P), z2_mx, slice(0, V))
+            nc.scalar.activation(out=y[:, u, :], in_=y_bank[:], func=COPY, scale=0.0625)
+            if u % 2:
+                nc.sync.dma_start(out=out_rows[:, u - 1 : u + 1, :], in_=y[:, u - 1 : u + 1, :])
         y_bf = [sbuf("y_bf%d" % h, [P, P * PACK], BF16) for h in range(2)]
-        nc.scalar.activation(out=y[0][:], in_=y_banks[0][:], func=COPY, scale=0.0625)
-        nc.vector.tensor_scalar(
-            out=y_bf[1][:].rearrange("p (v u) -> p v u", u=PACK),
-            in0=y_banks[1][:].rearrange("p u v -> p v u"),
-            scalar1=0.0625,
-            scalar2=None,
-            op0=MULT,
-        )
-        nc.scalar.activation(out=y[1][:], in_=y_banks[1][:], func=COPY, scale=0.0625)
-        weave(nc.vector.tensor_copy, y_bf[0][:], y[0][:])
         for h in range(2):
-            nc.sync.dma_start(out=out_rows[:, :, cols(h, P)], in_=y[h][:])
-        for h in (1, 0):
+            weave(nc.vector.tensor_copy, y_bf[h][:], y[:, :, cols(h, P)])
+        for h in range(2):
             quantize(y_codes, y_scale, cols(h, P), y_bf[h][:])
 
         nc.sync.dma_start(out=out_1[0].rearrange("p c r -> p (c r)").bitcast(I32), in_=y_codes[:].bitcast(I32))

@@ -1,7 +1,6 @@
 from contextlib import ExitStack
 
 import concourse.mybir as mybir
-from concourse.masks import make_identity
 
 K, T, S, V, H = 512, 2048, 512, 256, 512
 FLOPS = 2 * (2 * S * K * H + S * H * V)
@@ -18,7 +17,6 @@ MULT = mybir.AluOpType.mult
 
 P = 128
 PACK = 4
-RUN = 8
 HALF = H // 2
 QUARTER = H // 4
 
@@ -62,12 +60,10 @@ def tile_picked_gramsel_none_po_kernel(tc, x_words, x_scales, wa, wb, gt, gi, of
         feature_lists = sbuf("feature_lists", [P, V // 16], U16)
         all_words = sbuf("all_words", [P, T], I32)
         all_scales = sbuf("all_scales", [P, T], U8)
-        gate_rows = sbuf("gate_rows", [P, P], F32)
-        identity = sbuf("identity", [P, P], F32)
+        gt_sb = sbuf("gt_sb", [P, PACK], F32)
+        gi_sb = sbuf("gi_sb", [P, PACK], F32)
 
         nc.vector.memset(all_scales[:].bitcast(I32), 0)
-        nc.gpsimd.memset(gate_rows[:], 0.0)
-        make_identity(nc, identity[:])
 
         wa_raw = [sbuf("wa_raw%d" % h, [P, PACK, HALF], F32) for h in range(2)]
         wb_raw = [sbuf("wb_raw%d" % h, [P, PACK, HALF], F32) for h in range(2)]
@@ -76,51 +72,43 @@ def tile_picked_gramsel_none_po_kernel(tc, x_words, x_scales, wa, wb, gt, gi, of
             nc.sync.dma_start(out=tile[:], in_=w.rearrange("(p t) n -> p t n", t=PACK)[:, :, cols(h, HALF)])
 
         nc.sync.dma_start(token_list[:], offs)
-        nc.sync.dma_start(out=all_words[:], in_=x_words[0].rearrange("p c r -> p (c r)").bitcast(I32))
+        load_half(wa_raw[0], wa, 0)
         for q in range(4):
             nc.sync.dma_start(
                 out=all_scales[32 * q : 32 * q + 4, :].bitcast(I32),
                 in_=x_scales[0, 4 * q : 4 * q + 4, :].bitcast(I32),
             )
-        for first_row, gate in ((0, gt), (PACK, gi)):
-            nc.sync.dma_start(
-                out=gate_rows[first_row : first_row + PACK, :].rearrange("t (b r) -> t b r", r=RUN),
-                in_=gate.rearrange("(b t r) o -> t b (r o)", t=PACK, r=RUN),
-            )
-        for h in range(2):
-            load_half(wa_raw[h], wa, h)
+        nc.sync.dma_start(out=all_words[:], in_=x_words[0].rearrange("p c r -> p (c r)").bitcast(I32))
+        load_half(wa_raw[1], wa, 1)
+        nc.sync.dma_start(out=gi_sb[:], in_=gi.rearrange("(p t) o -> p (t o)", t=PACK))
         for h in range(2):
             load_half(wb_raw[h], wb, h)
         nc.sync.dma_start(feature_lists[:], fa)
-
-        gate_bank = bank(7, "gate_bank", [P, P])
-        nc.tensor.transpose(gate_bank[:], gate_rows[:], identity[:])
-        gates = sbuf("gates", [P, 2 * PACK], F32)
-        nc.scalar.copy(out=gates[:], in_=gate_bank[:, 0 : 2 * PACK])
-
-        x_codes = sbuf("x_codes", [P, S], U32)
-        picked_scales = sbuf("picked_scales", [P, S], U8)
-        x_scale = sbuf("x_scale", [P, S], U8)
-        nc.vector.tensor_copy(
-            out=x_codes[:].rearrange("p (t b r) -> p b t r", t=PACK, r=RUN),
-            in_=all_words[:].bitcast(U32).indirect(token_list[:]),
-        )
-        nc.vector.tensor_copy(out=picked_scales[:], in_=all_scales[:].indirect(token_list[:]))
-        nc.vector.tensor_copy(
-            out=x_scale[:].bitcast(I32).rearrange("p (t b r) -> p t b r", t=PACK, r=RUN // 4),
-            in_=picked_scales[:].bitcast(I32).rearrange("p (b t r) -> p t b r", t=PACK, r=RUN // 4),
-        )
-        x_mx = (x_codes, x_scale)
+        nc.sync.dma_start(out=gt_sb[:], in_=gt.rearrange("(p t) o -> p (t o)", t=PACK))
 
         wa_mx = (sbuf("wa_codes", [P, H], U32), sbuf("wa_scale", [P, H], U8))
         wb_mx = (sbuf("wb_codes", [P, H], U32), sbuf("wb_scale", [P, H], U8))
         wa_first = sbuf("wa_first", [P, HALF * PACK], BF16)
         wa_third = sbuf("wa_third", [P, QUARTER * PACK], BF16)
         wa_fourth = sbuf("wa_fourth", [P, QUARTER * PACK], BF16)
+        x_codes = sbuf("x_codes", [P, S], U32)
+        picked_scales = sbuf("picked_scales", [P, S], U8)
+        x_scale = sbuf("x_scale", [P, S], U8)
+        x_mx = (x_codes, x_scale)
+
         weave(nc.scalar.copy, wa_first[:], wa_raw[0][:])
+        nc.vector.tensor_copy(out=picked_scales[:], in_=all_scales[:].indirect(token_list[:]))
+        quantize(*wa_mx, cols(0, HALF), wa_first[:])
+        nc.vector.tensor_copy(
+            out=x_scale[:].rearrange("p (t m) -> p t m", t=PACK),
+            in_=picked_scales[:].rearrange("p (m t) -> p t m", t=PACK),
+        )
+        nc.vector.tensor_copy(
+            out=x_codes[:].rearrange("p (t m) -> p m t", t=PACK),
+            in_=all_words[:].bitcast(U32).indirect(token_list[:]),
+        )
         weave(nc.vector.tensor_copy, wa_third[:], wa_raw[1][:, :, cols(0, QUARTER)])
         weave(nc.scalar.copy, wa_fourth[:], wa_raw[1][:, :, cols(1, QUARTER)])
-        quantize(*wa_mx, cols(0, HALF), wa_first[:])
         quantize(*wa_mx, cols(2, QUARTER), wa_third[:])
         quantize(*wa_mx, cols(3, QUARTER), wa_fourth[:])
 
@@ -129,27 +117,26 @@ def tile_picked_gramsel_none_po_kernel(tc, x_words, x_scales, wa, wb, gt, gi, of
             a_bank = bank(t, "a_bank%d" % t, [P, H])
             product(a_bank[:], x_mx, cols(t, P), wa_mx, slice(0, H))
             a_row = sbuf("a_row%d" % t, [P, H], F32)
-            nc.scalar.activation(out=a_row[:], in_=a_bank[:], func=COPY, scale=gates[:, PACK + t : PACK + t + 1])
+            nc.scalar.activation(out=a_row[:], in_=a_bank[:], func=COPY, scale=gi_sb[:, t : t + 1])
             a_rows.append(a_row)
 
-        wb_first = sbuf("wb_first", [P, QUARTER * PACK], BF16)
-        wb_second = sbuf("wb_second", [P, QUARTER * PACK], BF16, "wa_fourth")
-        wb_last = sbuf("wb_last", [P, HALF * PACK], BF16)
-        weave(nc.scalar.copy, wb_first[:], wb_raw[0][:, :, cols(0, QUARTER)])
-        weave(nc.vector.tensor_copy, wb_second[:], wb_raw[0][:, :, cols(1, QUARTER)])
-        quantize(*wb_mx, cols(0, QUARTER), wb_first[:])
-        quantize(*wb_mx, cols(1, QUARTER), wb_second[:])
-        weave(nc.vector.tensor_copy, wb_last[:], wb_raw[1][:])
-        quantize(*wb_mx, cols(1, HALF), wb_last[:])
+        for h in range(2):
+            wb_bf = [sbuf("wb_bf%d%d" % (h, pair), [P, QUARTER * PACK], BF16) for pair in range(2)]
+            for pair in range(2):
+                nc.vector.tensor_copy(
+                    out=wb_bf[pair][:].rearrange("p (e m t) -> p m t e", e=2, t=PACK),
+                    in_=wb_raw[h][:].rearrange("p t (m u) -> p m t u", u=PACK)[:, :, :, cols(pair, 2)],
+                )
+            for pair in range(2):
+                quantize(*wb_mx, cols(2 * h + pair, QUARTER), wb_bf[pair][:])
 
-        pair_banks = [bank(PACK + pair, "pair_bank%d" % pair, [P, 2, HALF]) for pair in range(2)]
+        first_banks = [bank(PACK + n, "first_bank%d" % n, [P, 2, HALF]) for n in range(2)]
         for t in range(PACK):
-            product(pair_banks[t // 2][:, t % 2, :], x_mx, cols(t, P), wb_mx, cols(0, HALF))
-        quarter_banks = {}
-        for c in (2, 3):
-            quarter_banks[c] = bank(PACK + c, "quarter_bank%d" % c, [P, PACK, QUARTER])
+            product(first_banks[t // 2][:, t % 2, :], x_mx, cols(t, P), wb_mx, cols(0, HALF))
+        second_banks = [bank(PACK + 2 + pair, "second_bank%d" % pair, [P, PACK, QUARTER]) for pair in range(2)]
+        for pair in range(2):
             for t in range(PACK):
-                product(quarter_banks[c][:, t, :], x_mx, cols(t, P), wb_mx, cols(c, QUARTER))
+                product(second_banks[pair][:, t, :], x_mx, cols(t, P), wb_mx, cols(2 + pair, QUARTER))
 
         z2_planes = sbuf("z2_planes", [P, PACK, V], BF16, "wb_raw1")
         for t in range(PACK):
@@ -157,35 +144,32 @@ def tile_picked_gramsel_none_po_kernel(tc, x_words, x_scales, wa, wb, gt, gi, of
         z_planes = sbuf("z_planes", [P, PACK, HALF], BF16, "a_row0")
         for t in range(PACK):
             nc.scalar.activation(
-                out=z_planes[:, t, :].rearrange("p (u m) -> p u m", u=PACK),
-                in_=pair_banks[t // 2][:, t % 2, :].rearrange("p (m u) -> p u m", u=PACK),
-                func=COPY,
-                scale=gates[:, t : t + 1],
+                out=z_planes[:, t, :], in_=first_banks[t // 2][:, t % 2, :], func=COPY, scale=gt_sb[:, t : t + 1]
             )
 
         z2_bf = sbuf("z2_bf", [P, V * PACK], BF16)
         weave(nc.scalar.copy, z2_bf[:], z2_planes[:])
 
-        z_bf = sbuf("z_bf", [P, H * PACK], BF16, "a_row3")
-        z_view = z_bf[:].rearrange("p (u m t) -> p u m t", u=PACK, t=PACK)
-        gt_spread = gates[:, 0:PACK].unsqueeze(1).unsqueeze(1).to_broadcast([P, PACK, QUARTER // PACK, PACK])
-        for c in (2, 3):
+        z2_mx = (sbuf("z2_codes", [P, V], U32), sbuf("z2_scale", [P, V], U8))
+        gt_spread = gt_sb[:].unsqueeze(1).unsqueeze(1).to_broadcast([P, 2, QUARTER // 2, PACK])
+        z_bf = [sbuf("z_bf0", [P, 2 * P * PACK], BF16, "a_row3"), sbuf("z_bf1", [P, 2 * P * PACK], BF16)]
+        z_views = [tile[:].rearrange("p (e h m t) -> p h e m t", e=2, h=2, t=PACK) for tile in z_bf]
+        for pair in range(2):
             nc.vector.tensor_tensor(
-                out=z_view[:, :, cols(c, QUARTER // PACK), :],
-                in0=quarter_banks[c][:].rearrange("p t (m u) -> p u m t", u=PACK),
+                out=z_views[pair][:, 1],
+                in0=second_banks[pair][:].rearrange("p t (e m) -> p e m t", e=2),
                 in1=gt_spread,
                 op=MULT,
             )
-        nc.vector.tensor_copy(
-            out=z_view[:, :, cols(0, HALF // PACK), :].rearrange("p u (c i) t -> p u c t i", i=4),
-            in_=z_planes[:].rearrange("p t (u c i) -> p u c t i", u=PACK, i=4),
-        )
-
-        z_mx = (sbuf("z_codes", [P, H], U32), sbuf("z_scale", [P, H], U8))
-        z2_mx = (sbuf("z2_codes", [P, V], U32), sbuf("z2_scale", [P, V], U8))
         quantize(*z2_mx, slice(0, V), z2_bf[:])
-        for u in range(PACK):
-            quantize(*z_mx, cols(u, P), z_bf[:, cols(u, P * PACK)])
+        z_mx = (sbuf("z_codes", [P, H], U32, "z2_bf"), sbuf("z_scale", [P, H], U8))
+        for pair, copy in enumerate((nc.vector.tensor_copy, nc.scalar.copy)):
+            copy(
+                out=z_views[pair][:, 0].rearrange("p e (c i) t -> p e c t i", i=4),
+                in_=z_planes[:, :, cols(pair, QUARTER)].rearrange("p t (e c i) -> p e c t i", e=2, i=4),
+            )
+            for e in range(2):
+                quantize(*z_mx, cols(2 * pair + e, P), z_bf[pair][:, cols(e, P * PACK)])
 
         y_codes = sbuf("y_codes", [P, V], U32)
         y_scale = sbuf("y_scale", [P, V], U8)
@@ -198,8 +182,9 @@ def tile_picked_gramsel_none_po_kernel(tc, x_words, x_scales, wa, wb, gt, gi, of
             if u % 2:
                 nc.sync.dma_start(out=out_rows[:, u - 1 : u + 1, :], in_=y[:, u - 1 : u + 1, :])
         y_bf = [sbuf("y_bf%d" % h, [P, P * PACK], BF16) for h in range(2)]
-        for h in range(2):
-            weave(nc.vector.tensor_copy, y_bf[h][:], y[:, :, cols(h, P)])
+        weave(nc.vector.tensor_copy, y_bf[0][:], y[:, :, cols(0, P)])
+        weave(nc.vector.tensor_copy, y_bf[1][:, cols(0, 2 * P)], y[:, :, cols(2, P // 2)])
+        weave(nc.scalar.copy, y_bf[1][:, cols(1, 2 * P)], y[:, :, cols(3, P // 2)])
         for h in range(2):
             quantize(y_codes, y_scale, cols(h, P), y_bf[h][:])
 

from contextlib import ExitStack

import concourse.mybir as mybir

K, T, S, V, H = 512, 2048, 512, 256, 512
FLOPS = 2 * (2 * S * K * H + S * H * V)

F32 = mybir.dt.float32
BF16 = mybir.dt.bfloat16
I32 = mybir.dt.int32
U32 = mybir.dt.uint32
U16 = mybir.dt.uint16
U8 = mybir.dt.uint8
FP8X4 = mybir.dt.float8_e4m3fn_x4
COPY = mybir.ActivationFunctionType.Copy
MULT = mybir.AluOpType.mult

P = 128
PACK = 4
HALF = H // 2
QUARTER = H // 4


def tile_picked_gramsel_none_po_kernel(tc, x_words, x_scales, wa, wb, gt, gi, offs, fa, out_0, out_1, out_2):
    nc = tc.nc
    with ExitStack() as ctx:
        sb = ctx.enter_context(tc.tile_pool(name="sb", bufs=1))
        psum = ctx.enter_context(tc.psum_pool(name="psum", bufs=1))

        def sbuf(name, shape, dtype, tag=None):
            return sb.tile(shape, dtype, name=name, tag=tag or name, align_bytes=64)

        def bank(number, name, shape):
            return psum.tile(shape, F32, name=name, tag="bank%d" % number)

        def quantize(codes, scales, cols, values):
            nc.vector.quantize_mx(out=codes[:, cols].bitcast(FP8X4), scales=scales[:, cols], in_=values)

        def product(out, lhs, lhs_cols, rhs, rhs_cols):
            nc.tensor.matmul_mx(
                out=out,
                lhsT=lhs[0][:, lhs_cols].bitcast(FP8X4),
                lhsT_scale=lhs[1][:, lhs_cols],
                rhs=rhs[0][:, rhs_cols].bitcast(FP8X4),
                rhs_scale=rhs[1][:, rhs_cols],
                start=True,
                stop=True,
            )

        def weave(copy, dst, src):
            copy(
                out=dst.rearrange("p (c i t) -> p c t i", i=4, t=PACK),
                in_=src.rearrange("p t (c i) -> p c t i", i=4),
            )

        def cols(number, width):
            return slice(number * width, (number + 1) * width)

        token_list = sbuf("token_list", [P, S // 16], U16)
        feature_lists = sbuf("feature_lists", [P, V // 16], U16)
        all_words = sbuf("all_words", [P, T], I32)
        all_scales = sbuf("all_scales", [P, T], U8)
        gt_sb = sbuf("gt_sb", [P, PACK], F32)
        gi_sb = sbuf("gi_sb", [P, PACK], F32)

        nc.vector.memset(all_scales[:].bitcast(I32), 0)

        wa_raw = [sbuf("wa_raw%d" % h, [P, PACK, HALF], F32) for h in range(2)]
        wb_raw = [sbuf("wb_raw%d" % h, [P, PACK, HALF], F32) for h in range(2)]

        def load_half(tile, w, h):
            nc.sync.dma_start(out=tile[:], in_=w.rearrange("(p t) n -> p t n", t=PACK)[:, :, cols(h, HALF)])

        nc.sync.dma_start(token_list[:], offs)
        load_half(wa_raw[0], wa, 0)
        for q in range(4):
            nc.sync.dma_start(
                out=all_scales[32 * q : 32 * q + 4, :].bitcast(I32),
                in_=x_scales[0, 4 * q : 4 * q + 4, :].bitcast(I32),
            )
        nc.sync.dma_start(out=all_words[:], in_=x_words[0].rearrange("p c r -> p (c r)").bitcast(I32))
        load_half(wa_raw[1], wa, 1)
        nc.sync.dma_start(out=gi_sb[:], in_=gi.rearrange("(p t) o -> p (t o)", t=PACK))
        for h in range(2):
            load_half(wb_raw[h], wb, h)
        nc.sync.dma_start(feature_lists[:], fa)
        nc.sync.dma_start(out=gt_sb[:], in_=gt.rearrange("(p t) o -> p (t o)", t=PACK))

        wa_mx = (sbuf("wa_codes", [P, H], U32), sbuf("wa_scale", [P, H], U8))
        wb_mx = (sbuf("wb_codes", [P, H], U32), sbuf("wb_scale", [P, H], U8))
        wa_first = sbuf("wa_first", [P, HALF * PACK], BF16)
        wa_third = sbuf("wa_third", [P, QUARTER * PACK], BF16)
        wa_fourth = sbuf("wa_fourth", [P, QUARTER * PACK], BF16)
        x_codes = sbuf("x_codes", [P, S], U32)
        picked_scales = sbuf("picked_scales", [P, S], U8)
        x_scale = sbuf("x_scale", [P, S], U8)
        x_mx = (x_codes, x_scale)

        weave(nc.scalar.copy, wa_first[:], wa_raw[0][:])
        nc.vector.tensor_copy(out=picked_scales[:], in_=all_scales[:].indirect(token_list[:]))
        quantize(*wa_mx, cols(0, HALF), wa_first[:])
        nc.vector.tensor_copy(
            out=x_scale[:].rearrange("p (t m) -> p t m", t=PACK),
            in_=picked_scales[:].rearrange("p (m t) -> p t m", t=PACK),
        )
        nc.vector.tensor_copy(
            out=x_codes[:].rearrange("p (t m) -> p m t", t=PACK),
            in_=all_words[:].bitcast(U32).indirect(token_list[:]),
        )
        weave(nc.vector.tensor_copy, wa_third[:], wa_raw[1][:, :, cols(0, QUARTER)])
        weave(nc.scalar.copy, wa_fourth[:], wa_raw[1][:, :, cols(1, QUARTER)])
        quantize(*wa_mx, cols(2, QUARTER), wa_third[:])
        quantize(*wa_mx, cols(3, QUARTER), wa_fourth[:])

        a_rows = []
        for t in range(PACK):
            a_bank = bank(t, "a_bank%d" % t, [P, H])
            product(a_bank[:], x_mx, cols(t, P), wa_mx, slice(0, H))
            a_row = sbuf("a_row%d" % t, [P, H], F32)
            nc.scalar.activation(out=a_row[:], in_=a_bank[:], func=COPY, scale=gi_sb[:, t : t + 1])
            a_rows.append(a_row)

        for h in range(2):
            wb_bf = [sbuf("wb_bf%d%d" % (h, pair), [P, QUARTER * PACK], BF16) for pair in range(2)]
            for pair in range(2):
                nc.vector.tensor_copy(
                    out=wb_bf[pair][:].rearrange("p (e m t) -> p m t e", e=2, t=PACK),
                    in_=wb_raw[h][:].rearrange("p t (m u) -> p m t u", u=PACK)[:, :, :, cols(pair, 2)],
                )
            for pair in range(2):
                quantize(*wb_mx, cols(2 * h + pair, QUARTER), wb_bf[pair][:])

        first_banks = [bank(PACK + n, "first_bank%d" % n, [P, 2, HALF]) for n in range(2)]
        for t in range(PACK):
            product(first_banks[t // 2][:, t % 2, :], x_mx, cols(t, P), wb_mx, cols(0, HALF))
        second_banks = [bank(PACK + 2 + pair, "second_bank%d" % pair, [P, PACK, QUARTER]) for pair in range(2)]
        for pair in range(2):
            for t in range(PACK):
                product(second_banks[pair][:, t, :], x_mx, cols(t, P), wb_mx, cols(2 + pair, QUARTER))

        z2_planes = sbuf("z2_planes", [P, PACK, V], BF16, "wb_raw1")
        for t in range(PACK):
            nc.vector.tensor_copy(out=z2_planes[:, t, :], in_=a_rows[t][:].indirect(feature_lists[:]))
        z_planes = sbuf("z_planes", [P, PACK, HALF], BF16, "a_row0")
        for t in range(PACK):
            nc.scalar.activation(
                out=z_planes[:, t, :], in_=first_banks[t // 2][:, t % 2, :], func=COPY, scale=gt_sb[:, t : t + 1]
            )

        z2_bf = sbuf("z2_bf", [P, V * PACK], BF16)
        weave(nc.scalar.copy, z2_bf[:], z2_planes[:])

        z2_mx = (sbuf("z2_codes", [P, V], U32), sbuf("z2_scale", [P, V], U8))
        gt_spread = gt_sb[:].unsqueeze(1).unsqueeze(1).to_broadcast([P, 2, QUARTER // 2, PACK])
        z_bf = [sbuf("z_bf0", [P, 2 * P * PACK], BF16, "a_row3"), sbuf("z_bf1", [P, 2 * P * PACK], BF16)]
        z_views = [tile[:].rearrange("p (e h m t) -> p h e m t", e=2, h=2, t=PACK) for tile in z_bf]
        for pair in range(2):
            nc.vector.tensor_tensor(
                out=z_views[pair][:, 1],
                in0=second_banks[pair][:].rearrange("p t (e m) -> p e m t", e=2),
                in1=gt_spread,
                op=MULT,
            )
        quantize(*z2_mx, slice(0, V), z2_bf[:])
        z_mx = (sbuf("z_codes", [P, H], U32, "z2_bf"), sbuf("z_scale", [P, H], U8))
        for pair, copy in enumerate((nc.vector.tensor_copy, nc.scalar.copy)):
            copy(
                out=z_views[pair][:, 0].rearrange("p e (c i) t -> p e c t i", i=4),
                in_=z_planes[:, :, cols(pair, QUARTER)].rearrange("p t (e c i) -> p e c t i", e=2, i=4),
            )
            for e in range(2):
                quantize(*z_mx, cols(2 * pair + e, P), z_bf[pair][:, cols(e, P * PACK)])

        y_codes = sbuf("y_codes", [P, V], U32)
        y_scale = sbuf("y_scale", [P, V], U8)
        out_rows = out_0.rearrange("(p u) v -> p u v", u=PACK)
        y = sbuf("y", [P, PACK, V], F32)
        for u in range(PACK):
            y_bank = bank(u, "y_bank%d" % u, [P, V])
            product(y_bank[:], z_mx, cols(u, P), z2_mx, slice(0, V))
            nc.scalar.activation(out=y[:, u, :], in_=y_bank[:], func=COPY, scale=0.0625)
            if u % 2:
                nc.sync.dma_start(out=out_rows[:, u - 1 : u + 1, :], in_=y[:, u - 1 : u + 1, :])
        y_bf = [sbuf("y_bf%d" % h, [P, P * PACK], BF16) for h in range(2)]
        weave(nc.vector.tensor_copy, y_bf[0][:], y[:, :, cols(0, P)])
        weave(nc.vector.tensor_copy, y_bf[1][:, cols(0, 2 * P)], y[:, :, cols(2, P // 2)])
        weave(nc.scalar.copy, y_bf[1][:, cols(1, 2 * P)], y[:, :, cols(3, P // 2)])
        for h in range(2):
            quantize(y_codes, y_scale, cols(h, P), y_bf[h][:])

        nc.sync.dma_start(out=out_1[0].rearrange("p c r -> p (c r)").bitcast(I32), in_=y_codes[:].bitcast(I32))
        for q in range(4):
            queue = nc.scalar if q % 2 else nc.sync
            queue.dma_start(
                out=out_2[0, 4 * q : 4 * q + 4, :].bitcast(I32),
                in_=y_scale[32 * q : 32 * q + 4, :].bitcast(I32),
            )
